import numpy as np
import ml_dtypes


def mxq(x, axis, fmt="e4m3"):
    dtype, down = {"e4m3": (ml_dtypes.float8_e4m3fn, 7), "e5m2": (ml_dtypes.float8_e5m2, 14)}[fmt]
    v = np.moveaxis(np.asarray(x, np.float32).astype(ml_dtypes.bfloat16).astype(np.float64), axis, -1)
    blocks = v.reshape(v.shape[:-1] + (-1, 32))
    amax = np.abs(blocks).max(-1, keepdims=True)
    byte = np.maximum(np.where(amax > 0, np.frexp(amax)[1] - 1 + 127, 0) - down, 1)
    scale = np.exp2(byte - 127.0)
    codes = (blocks / scale).astype(np.float32).astype(dtype).astype(np.float64)
    return np.moveaxis((codes * scale).reshape(v.shape), -1, axis)


WIDE = False


def mx_kscale(k):
    if not WIDE:
        return np.ones(k)
    levels = np.array([30, -30])
    if k % 512:
        return np.exp2(np.random.permutation(np.resize(levels, k // 32))).repeat(32)
    a = np.empty((k // 512, 16))
    for p in range(k // 512):
        a[p, :8] = np.random.permutation(np.resize(levels, 8))
        for g in range(8):
            far = levels[np.abs(levels - a[p, g]) >= 10]
            a[p, g + 8] = far[np.random.randint(len(far))]
    return np.exp2(a.ravel()).repeat(32)


def f64(x):
    return np.asarray(x).astype(np.float64)


def striped(idx):
    return np.tile(np.asarray(idx).reshape(-1, 16).T, (8, 1)).astype(np.uint16)


def unstriped(offs):
    return offs[:16].T.reshape(-1).astype(np.int64)


E2M1 = np.array([0.0, 0.5, 1.0, 1.5, 2.0, 3.0, 4.0, 6.0, -0.0, -0.5, -1.0, -1.5, -2.0, -3.0, -4.0, -6.0])


def pack_weight(w, fmt):
    k, n = w.shape
    w = f64(np.asarray(w, np.float32).astype(ml_dtypes.bfloat16)).reshape(k // 32, 32, n)
    amax = np.abs(w).max(1)
    if fmt in ("e4m3", "e5m2"):
        byte = np.frexp(amax)[1] - 1 + 127 - (7 if fmt == "e4m3" else 14)
    else:
        mant, ex = np.frexp(amax / 6.0)
        byte = np.where(mant > 0.5, ex, ex - 1) + 127
    byte = np.clip(np.where(amax > 0, byte, 1), 1, 254)
    scaled = (w * np.exp2(127.0 - byte)[:, None, :]).reshape(k, n).astype(np.float32)
    by_word = np.ascontiguousarray(scaled.reshape(k // 512, 128, 4, n).transpose(0, 1, 3, 2))
    if fmt in ("e4m3", "e5m2"):
        words = by_word.astype(ml_dtypes.float8_e4m3fn if fmt == "e4m3" else ml_dtypes.float8_e5m2).view(np.uint8)
    else:
        c = by_word.astype(ml_dtypes.float4_e2m1fn).view(np.uint8) & 0xF
        words = (c[..., 0::2] | (c[..., 1::2] << 4)).reshape(k // 512, 128, 2 * n)
    return np.ascontiguousarray(words), np.ascontiguousarray(byte.astype(np.uint8).reshape(k // 512, 16, n))


def unpack_weight(words, scales, fmt):
    g, _, n = scales.shape
    words = np.ascontiguousarray(words).reshape(g, 128, n, -1)
    if fmt in ("e4m3", "e5m2"):
        vals = words.view(ml_dtypes.float8_e4m3fn if fmt == "e4m3" else ml_dtypes.float8_e5m2).astype(np.float64)
    else:
        nib = np.empty((g, 128, n, 4), np.uint8)
        nib[..., 0::2] = words & 0xF
        nib[..., 1::2] = words >> 4
        vals = E2M1[nib]
    vals = vals * np.repeat(np.exp2(scales.astype(np.float64) - 127.0), 8, axis=1)[..., None]
    return vals.transpose(0, 1, 3, 2).reshape(g * 512, n)


K, T, J, N = 1024, 1024, 256, 256


def setup_inputs():
    n = np.random.standard_normal
    idx = np.random.permutation(T)[:J]
    idx2 = np.random.permutation(T)[:J]
    fk = mx_kscale(K)
    xtp = pack_weight(n((K, T)) * np.random.uniform(0.4, 1.6, (1, T)) / fk[:, None], "e5m2")
    wap = pack_weight(n((K, N)) * 1 / np.sqrt(K) * fk[:, None], "e5m2")
    return {
        "xt_words": xtp[0],
        "xt_scales": xtp[1],
        "wa_words": wap[0],
        "wa_scales": wap[1],
        "wb": (n((K, N)) * 1 / np.sqrt(K) * fk[:, None]).astype(np.float32),
        "bi": (np.random.uniform(-0.6, 0.6, (1, N))).astype(np.float32),
        "offs": striped(idx),
        "offs2": striped(idx2),
    }


def reference(xt_words, xt_scales, wa_words, wa_scales, wb, bi, offs, offs2):
    idx = unstriped(offs)
    idx2 = unstriped(offs2)
    xtu = unpack_weight(xt_words, xt_scales, "e5m2")
    wau = unpack_weight(wa_words, wa_scales, "e5m2")
    xtidxg = xtu[:, idx]
    a = xtidxg.T @ wau
    xtidx2g = xtu[:, idx2]
    wbq = mxq(f64(wb), 0, "e4m3")
    b0 = xtidx2g.T @ wbq
    b2 = b0 + f64(bi)
    e = np.exp(0.6 * (a - b2))
    y = 256.0 * e / np.sum(e, axis=1, keepdims=True)
    return y

@@ -1,0 +1,148 @@
+from contextlib import ExitStack
+
+import concourse.mybir as mybir
+from concourse.masks import make_identity
+
+K, T, J, N = 1024, 1024, 256, 256
+FLOPS = 2 * 2 * J * K * N
+
+F32 = mybir.dt.float32
+BF16 = mybir.dt.bfloat16
+I32 = mybir.dt.int32
+U32 = mybir.dt.uint32
+U16 = mybir.dt.uint16
+U8 = mybir.dt.uint8
+E4M3 = mybir.dt.float8_e4m3fn_x4
+E5M2 = mybir.dt.float8_e5m2_x4
+ALU = mybir.AluOpType
+ACT = mybir.ActivationFunctionType
+
+P = 128
+PACK = 4
+PASSES = K // (P * PACK)
+JT = J // P
+
+
+def load_planes(nc, planes, scales):
+    for q in range(4):
+        nc.sync.dma_start(
+            out=planes[32 * q : 32 * q + 4, :, :].bitcast(I32),
+            in_=scales[:, 4 * q : 4 * q + 4, :].rearrange("z r c -> r z c").bitcast(I32),
+        )
+
+
+def tile_list_rows_twotokens_sharesofgap_kernel(
+    tc, xt_words, xt_scales, wa_words, wa_scales, wb, bi, offs, offs2, out
+):
+    nc = tc.nc
+    with ExitStack() as ctx:
+        sb = ctx.enter_context(tc.tile_pool(name="sb", bufs=1))
+        ps = ctx.enter_context(tc.psum_pool(name="ps", bufs=1))
+
+        lists = [sb.tile([P, J // 16], U16, name=f"list{a}") for a in range(2)]
+        xs = sb.tile([P, PASSES, T], U8, name="xs", align_bytes=64)
+        xw = [sb.tile([P, T], U32, name=f"xw{z}", align_bytes=64) for z in range(PASSES)]
+        wb_raw = [sb.tile([P, PACK, N], F32, name=f"wb_raw{z}") for z in range(PASSES)]
+        wa_w = sb.tile([P, PASSES, N], U32, name="wa_w", align_bytes=64)
+        wa_s = sb.tile([P, PASSES, N], U8, name="wa_s", align_bytes=64)
+        bi_col = sb.tile([P, 2], F32, name="bi_col")
+
+        def load_xw(z):
+            nc.sync.dma_start(out=xw[z][:].bitcast(I32), in_=xt_words[z].rearrange("p c r -> p (c r)").bitcast(I32))
+
+        def load_wb(z):
+            rows = wb[z * P * PACK : (z + 1) * P * PACK, :]
+            nc.sync.dma_start(out=wb_raw[z][:], in_=rows.rearrange("(p t) n -> p t n", t=PACK))
+
+        nc.vector.memset(xs[:].bitcast(I32), 0)
+        nc.vector.memset(wa_s[:].bitcast(I32), 0)
+        load_xw(0)
+        nc.sync.dma_start(out=lists[0][:], in_=offs)
+        nc.sync.dma_start(out=lists[1][:], in_=offs2)
+        load_planes(nc, xs, xt_scales)
+        load_wb(0)
+        load_wb(1)
+        load_xw(1)
+        nc.sync.dma_start(out=wa_w[:].bitcast(I32), in_=wa_words.rearrange("z p c r -> p z (c r)").bitcast(I32))
+        load_planes(nc, wa_s, wa_scales)
+        nc.sync.dma_start(out=bi_col[:], in_=bi.rearrange("o (p c) -> p (o c)", c=2))
+
+        ident = sb.tile([P, P], F32, name="ident")
+        make_identity(nc, ident[:])
+
+        gs = [[sb.tile([P, J], U8, name=f"gs{a}{z}", align_bytes=64) for z in range(PASSES)] for a in range(2)]
+        gw = [[sb.tile([P, J], U32, name=f"gw{a}{z}", align_bytes=64) for z in range(PASSES)] for a in range(2)]
+        wb_bf = [sb.tile([P, N, PACK], BF16, name=f"wb_bf{z}", align_bytes=64) for z in range(PASSES)]
+        wb_w = [sb.tile([P, N], U32, name=f"wb_w{z}", align_bytes=64) for z in range(PASSES)]
+        wb_s = [sb.tile([P, N], U8, name=f"wb_s{z}", align_bytes=64) for z in range(PASSES)]
+
+        for z in range(PASSES):
+            nc.scalar.activation(
+                out=wb_bf[z][:].rearrange("p (c i) t -> p c t i", i=4),
+                in_=wb_raw[z][:].rearrange("p t (c i) -> p c t i", i=4),
+                func=ACT.Copy,
+                scale=-1.0,
+            )
+
+        bi_ps = ps.tile([P, 2, P], F32, name="bi_ps")
+        for c in range(2):
+            nc.tensor.transpose(bi_ps[:, c, :], bi_col[:, c : c + 1].to_broadcast([P, P]), ident[:])
+        bi_row = sb.tile([P, P, 2], F32, name="bi_row")
+        nc.scalar.activation(out=bi_row[:], in_=bi_ps[:].rearrange("p c q -> p q c"), func=ACT.Copy, scale=0.6)
+
+        def quantize(z):
+            nc.vector.quantize_mx(
+                out=wb_w[z][:].bitcast(E4M3), scales=wb_s[z][:], in_=wb_bf[z][:].rearrange("p n t -> p (n t)")
+            )
+
+        for a in range(2):
+            nc.vector.tensor_copy(out=gw[a][0][:], in_=xw[0][:].indirect(lists[a][:]))
+        for z in range(PASSES):
+            for a in range(2):
+                nc.vector.tensor_copy(out=gs[a][z][:], in_=xs[:, z, :].indirect(lists[a][:]))
+        quantize(0)
+        quantize(1)
+        for jt in range(JT):
+            for a in range(2):
+                nc.vector.tensor_copy(
+                    out=gw[a][1][:, jt * P : (jt + 1) * P], in_=xw[1][:].indirect(lists[a][:, jt * 8 : (jt + 1) * 8])
+                )
+
+        acc = [ps.tile([P, N], F32, name=f"acc{jt}") for jt in range(JT)]
+
+        def product(jt, a, z, start, stop):
+            cols = slice(jt * P, (jt + 1) * P)
+            if a == 0:
+                rhs, rhs_scale = wa_w[:, z, :].bitcast(E5M2), wa_s[:, z, :]
+            else:
+                rhs, rhs_scale = wb_w[z][:].bitcast(E4M3), wb_s[z][:]
+            nc.tensor.matmul_mx(
+                out=acc[jt][:], lhsT=gw[a][z][:, cols].bitcast(E5M2), lhsT_scale=gs[a][z][:, cols],
+                rhs=rhs, rhs_scale=rhs_scale, start=start, stop=stop,
+            )
+
+        for jt in range(JT):
+            product(jt, 1, 0, True, False)
+        for jt in range(JT):
+            product(jt, 0, 0, False, False)
+        for jt in range(JT):
+            product(jt, 0, 1, False, False)
+            product(jt, 1, 1, False, True)
+
+        for jt in range(JT):
+            neg = sb.tile([P, N], F32, name=f"neg{jt}")
+            low = sb.tile([P, 1], F32, name=f"low{jt}")
+            e = sb.tile([P, N], F32, name=f"e{jt}")
+            total = sb.tile([P, 1], F32, name=f"total{jt}")
+            inv = sb.tile([P, 1], F32, name=f"inv{jt}")
+            y = sb.tile([P, N], F32, name=f"y{jt}")
+            nc.vector.scalar_tensor_tensor(
+                out=neg[:], in0=acc[jt][:], scalar=-0.6, in1=bi_row[:].rearrange("p q c -> p (q c)"),
+                op0=ALU.mult, op1=ALU.add,
+            )
+            nc.vector.tensor_reduce(out=low[:], in_=neg[:], axis=mybir.AxisListType.X, op=ALU.min)
+            nc.scalar.activation(out=e[:], in_=neg[:], func=ACT.Exp, bias=low[:], scale=-1.0, accum_out=total[:])
+            nc.vector.reciprocal(out=inv[:], in_=total[:])
+            nc.vector.tensor_scalar(out=y[:], in0=e[:], scalar1=inv[:], scalar2=256.0, op0=ALU.mult, op1=ALU.mult)
+            queue = nc.sync if jt == 0 else nc.scalar
+            queue.dma_start(out=out[jt * P : (jt + 1) * P, :], in_=y[:])

@@ -47,8 +47,8 @@ def tile_list_rows_twotokens_sharesofgap_kernel(
         wa_s = sb.tile([P, PASSES, N], U8, name="wa_s", align_bytes=64)
         bi_col = sb.tile([P, 2], F32, name="bi_col")
 
-        def load_xw(z):
-            nc.sync.dma_start(out=xw[z][:].bitcast(I32), in_=xt_words[z].rearrange("p c r -> p (c r)").bitcast(I32))
+        def load_xw(z, queue):
+            queue.dma_start(out=xw[z][:].bitcast(I32), in_=xt_words[z].rearrange("p c r -> p (c r)").bitcast(I32))
 
         def load_wb(z):
             rows = wb[z * P * PACK : (z + 1) * P * PACK, :]
@@ -56,16 +56,16 @@ def tile_list_rows_twotokens_sharesofgap_kernel(
 
         nc.vector.memset(xs[:].bitcast(I32), 0)
         nc.vector.memset(wa_s[:].bitcast(I32), 0)
-        load_xw(0)
+        nc.gpsimd.dma_start(out=bi_col[:], in_=bi.rearrange("o (p c) -> p (o c)", c=2))
+        load_xw(0, nc.scalar)
         nc.sync.dma_start(out=lists[0][:], in_=offs)
         nc.sync.dma_start(out=lists[1][:], in_=offs2)
         load_planes(nc, xs, xt_scales)
         load_wb(0)
         load_wb(1)
-        load_xw(1)
         nc.sync.dma_start(out=wa_w[:].bitcast(I32), in_=wa_words.rearrange("z p c r -> p z (c r)").bitcast(I32))
         load_planes(nc, wa_s, wa_scales)
-        nc.sync.dma_start(out=bi_col[:], in_=bi.rearrange("o (p c) -> p (o c)", c=2))
+        load_xw(1, nc.sync)
 
         ident = sb.tile([P, P], F32, name="ident")
         make_identity(nc, ident[:])
@@ -95,15 +95,15 @@ def tile_list_rows_twotokens_sharesofgap_kernel(
                 out=wb_w[z][:].bitcast(E4M3), scales=wb_s[z][:], in_=wb_bf[z][:].rearrange("p n t -> p (n t)")
             )
 
-        for a in range(2):
-            nc.vector.tensor_copy(out=gw[a][0][:], in_=xw[0][:].indirect(lists[a][:]))
         for z in range(PASSES):
             for a in range(2):
                 nc.vector.tensor_copy(out=gs[a][z][:], in_=xs[:, z, :].indirect(lists[a][:]))
+        for a in range(2):
+            nc.vector.tensor_copy(out=gw[a][0][:], in_=xw[0][:].indirect(lists[a][:]))
         quantize(0)
         quantize(1)
         for jt in range(JT):
-            for a in range(2):
+            for a in (1, 0):
                 nc.vector.tensor_copy(
                     out=gw[a][1][:, jt * P : (jt + 1) * P], in_=xw[1][:].indirect(lists[a][:, jt * 8 : (jt + 1) * 8])
                 )
@@ -126,8 +126,8 @@ def tile_list_rows_twotokens_sharesofgap_kernel(
         for jt in range(JT):
             product(jt, 0, 0, False, False)
         for jt in range(JT):
-            product(jt, 0, 1, False, False)
-            product(jt, 1, 1, False, True)
+            product(jt, 1, 1, False, False)
+            product(jt, 0, 1, False, True)
 
         for jt in range(JT):
             neg = sb.tile([P, N], F32, name=f"neg{jt}")

@@ -42,13 +42,16 @@ def tile_list_rows_twotokens_sharesofgap_kernel(
         lists = [sb.tile([P, J // 16], U16, name=f"list{a}") for a in range(2)]
         xs = sb.tile([P, PASSES, T], U8, name="xs", align_bytes=64)
         xw = [sb.tile([P, T], U32, name=f"xw{z}", align_bytes=64) for z in range(PASSES)]
-        wb_raw = [sb.tile([P, PACK, N], F32, name=f"wb_raw{z}") for z in range(PASSES)]
-        wa_w = sb.tile([P, PASSES, N], U32, name="wa_w", align_bytes=64)
+        wb_raw = [sb.tile([P, PACK, N], F32, name=f"wb_raw{z}", tag=f"wb_raw{z}", align_bytes=64) for z in range(PASSES)]
+        wa_w = [sb.tile([P, N], U32, name=f"wa_w{z}", align_bytes=64) for z in range(PASSES)]
         wa_s = sb.tile([P, PASSES, N], U8, name="wa_s", align_bytes=64)
         bi_col = sb.tile([P, 2], F32, name="bi_col")
 
         def load_xw(z, queue):
             queue.dma_start(out=xw[z][:].bitcast(I32), in_=xt_words[z].rearrange("p c r -> p (c r)").bitcast(I32))
+
+        def load_wa(z):
+            nc.sync.dma_start(out=wa_w[z][:].bitcast(I32), in_=wa_words[z].rearrange("p c r -> p (c r)").bitcast(I32))
 
         def load_wb(z):
             rows = wb[z * P * PACK : (z + 1) * P * PACK, :]
@@ -63,16 +66,17 @@ def tile_list_rows_twotokens_sharesofgap_kernel(
         load_planes(nc, xs, xt_scales)
         load_wb(0)
         load_wb(1)
-        nc.sync.dma_start(out=wa_w[:].bitcast(I32), in_=wa_words.rearrange("z p c r -> p z (c r)").bitcast(I32))
+        load_wa(0)
         load_planes(nc, wa_s, wa_scales)
         load_xw(1, nc.sync)
+        load_wa(1)
 
         ident = sb.tile([P, P], F32, name="ident")
         make_identity(nc, ident[:])
 
         gs = [[sb.tile([P, J], U8, name=f"gs{a}{z}", align_bytes=64) for z in range(PASSES)] for a in range(2)]
-        gw = [[sb.tile([P, J], U32, name=f"gw{a}{z}", align_bytes=64) for z in range(PASSES)] for a in range(2)]
-        wb_bf = [sb.tile([P, N, PACK], BF16, name=f"wb_bf{z}", align_bytes=64) for z in range(PASSES)]
+        gw = [sb.tile([P, 2, J], U32, name="gw0", align_bytes=64)]
+        wb_bf = [sb.tile([P, N, PACK], BF16, name=f"wb_bf{z}", tag=f"wb_bf{z}", align_bytes=64) for z in range(PASSES)]
         wb_w = [sb.tile([P, N], U32, name=f"wb_w{z}", align_bytes=64) for z in range(PASSES)]
         wb_s = [sb.tile([P, N], U8, name=f"wb_s{z}", align_bytes=64) for z in range(PASSES)]
 
@@ -87,8 +91,6 @@ def tile_list_rows_twotokens_sharesofgap_kernel(
         bi_ps = ps.tile([P, 2, P], F32, name="bi_ps")
         for c in range(2):
             nc.tensor.transpose(bi_ps[:, c, :], bi_col[:, c : c + 1].to_broadcast([P, P]), ident[:])
-        bi_row = sb.tile([P, P, 2], F32, name="bi_row")
-        nc.scalar.activation(out=bi_row[:], in_=bi_ps[:].rearrange("p c q -> p q c"), func=ACT.Copy, scale=0.6)
 
         def quantize(z):
             nc.vector.quantize_mx(
@@ -99,13 +101,16 @@ def tile_list_rows_twotokens_sharesofgap_kernel(
             for a in range(2):
                 nc.vector.tensor_copy(out=gs[a][z][:], in_=xs[:, z, :].indirect(lists[a][:]))
         for a in range(2):
-            nc.vector.tensor_copy(out=gw[a][0][:], in_=xw[0][:].indirect(lists[a][:]))
+            nc.vector.tensor_copy(out=gw[0][:, a, :], in_=xw[0][:].indirect(lists[a][:]))
         quantize(0)
+        bi_row = sb.tile([P, P, 2], F32, name="bi_row", tag="wb_bf0", align_bytes=64)
+        nc.scalar.activation(out=bi_row[:], in_=bi_ps[:].rearrange("p c q -> p q c"), func=ACT.Copy, scale=0.6)
         quantize(1)
+        gw.append(sb.tile([P, 2, J], U32, name="gw1", tag="wb_raw1", align_bytes=64))
         for jt in range(JT):
             for a in (1, 0):
                 nc.vector.tensor_copy(
-                    out=gw[a][1][:, jt * P : (jt + 1) * P], in_=xw[1][:].indirect(lists[a][:, jt * 8 : (jt + 1) * 8])
+                    out=gw[1][:, a, jt * P : (jt + 1) * P], in_=xw[1][:].indirect(lists[a][:, jt * 8 : (jt + 1) * 8])
                 )
 
         acc = [ps.tile([P, N], F32, name=f"acc{jt}") for jt in range(JT)]
@@ -113,18 +118,18 @@ def tile_list_rows_twotokens_sharesofgap_kernel(
         def product(jt, a, z, start, stop):
             cols = slice(jt * P, (jt + 1) * P)
             if a == 0:
-                rhs, rhs_scale = wa_w[:, z, :].bitcast(E5M2), wa_s[:, z, :]
+                rhs, rhs_scale = wa_w[z][:].bitcast(E5M2), wa_s[:, z, :]
             else:
                 rhs, rhs_scale = wb_w[z][:].bitcast(E4M3), wb_s[z][:]
             nc.tensor.matmul_mx(
-                out=acc[jt][:], lhsT=gw[a][z][:, cols].bitcast(E5M2), lhsT_scale=gs[a][z][:, cols],
+                out=acc[jt][:], lhsT=gw[z][:, a, cols].bitcast(E5M2), lhsT_scale=gs[a][z][:, cols],
                 rhs=rhs, rhs_scale=rhs_scale, start=start, stop=stop,
             )
 
         for jt in range(JT):
-            product(jt, 1, 0, True, False)
+            product(jt, 0, 0, True, False)
         for jt in range(JT):
-            product(jt, 0, 0, False, False)
+            product(jt, 1, 0, False, False)
         for jt in range(JT):
             product(jt, 1, 1, False, False)
             product(jt, 0, 1, False, True)

from contextlib import ExitStack

import concourse.mybir as mybir
from concourse.masks import make_identity

K, T, J, N = 1024, 1024, 256, 256
FLOPS = 2 * 2 * J * K * N

F32 = mybir.dt.float32
BF16 = mybir.dt.bfloat16
I32 = mybir.dt.int32
U32 = mybir.dt.uint32
U16 = mybir.dt.uint16
U8 = mybir.dt.uint8
E4M3 = mybir.dt.float8_e4m3fn_x4
E5M2 = mybir.dt.float8_e5m2_x4
ALU = mybir.AluOpType
ACT = mybir.ActivationFunctionType

P = 128
PACK = 4
PASSES = K // (P * PACK)
JT = J // P


def load_planes(nc, planes, scales):
    for q in range(4):
        nc.sync.dma_start(
            out=planes[32 * q : 32 * q + 4, :, :].bitcast(I32),
            in_=scales[:, 4 * q : 4 * q + 4, :].rearrange("z r c -> r z c").bitcast(I32),
        )


def tile_list_rows_twotokens_sharesofgap_kernel(
    tc, xt_words, xt_scales, wa_words, wa_scales, wb, bi, offs, offs2, out
):
    nc = tc.nc
    with ExitStack() as ctx:
        sb = ctx.enter_context(tc.tile_pool(name="sb", bufs=1))
        ps = ctx.enter_context(tc.psum_pool(name="ps", bufs=1))

        lists = [sb.tile([P, J // 16], U16, name=f"list{a}") for a in range(2)]
        xs = sb.tile([P, PASSES, T], U8, name="xs", align_bytes=64)
        xw = [sb.tile([P, T], U32, name=f"xw{z}", align_bytes=64) for z in range(PASSES)]
        wb_raw = [sb.tile([P, PACK, N], F32, name=f"wb_raw{z}", tag=f"wb_raw{z}", align_bytes=64) for z in range(PASSES)]
        wa_w = [sb.tile([P, N], U32, name=f"wa_w{z}", align_bytes=64) for z in range(PASSES)]
        wa_s = sb.tile([P, PASSES, N], U8, name="wa_s", align_bytes=64)
        bi_col = sb.tile([P, 2], F32, name="bi_col")

        def load_xw(z, queue):
            queue.dma_start(out=xw[z][:].bitcast(I32), in_=xt_words[z].rearrange("p c r -> p (c r)").bitcast(I32))

        def load_wa(z):
            nc.sync.dma_start(out=wa_w[z][:].bitcast(I32), in_=wa_words[z].rearrange("p c r -> p (c r)").bitcast(I32))

        def load_wb(z):
            rows = wb[z * P * PACK : (z + 1) * P * PACK, :]
            nc.sync.dma_start(out=wb_raw[z][:], in_=rows.rearrange("(p t) n -> p t n", t=PACK))

        nc.vector.memset(xs[:].bitcast(I32), 0)
        nc.vector.memset(wa_s[:].bitcast(I32), 0)
        nc.gpsimd.dma_start(out=bi_col[:], in_=bi.rearrange("o (p c) -> p (o c)", c=2))
        load_xw(0, nc.scalar)
        nc.sync.dma_start(out=lists[0][:], in_=offs)
        nc.sync.dma_start(out=lists[1][:], in_=offs2)
        load_planes(nc, xs, xt_scales)
        load_wb(0)
        load_wb(1)
        load_wa(0)
        load_planes(nc, wa_s, wa_scales)
        load_xw(1, nc.sync)
        load_wa(1)

        ident = sb.tile([P, P], F32, name="ident")
        make_identity(nc, ident[:])

        gs = [[sb.tile([P, J], U8, name=f"gs{a}{z}", align_bytes=64) for z in range(PASSES)] for a in range(2)]
        gw = [sb.tile([P, 2, J], U32, name="gw0", align_bytes=64)]
        wb_bf = [sb.tile([P, N, PACK], BF16, name=f"wb_bf{z}", tag=f"wb_bf{z}", align_bytes=64) for z in range(PASSES)]
        wb_w = [sb.tile([P, N], U32, name=f"wb_w{z}", align_bytes=64) for z in range(PASSES)]
        wb_s = [sb.tile([P, N], U8, name=f"wb_s{z}", align_bytes=64) for z in range(PASSES)]

        for z in range(PASSES):
            nc.scalar.activation(
                out=wb_bf[z][:].rearrange("p (c i) t -> p c t i", i=4),
                in_=wb_raw[z][:].rearrange("p t (c i) -> p c t i", i=4),
                func=ACT.Copy,
                scale=-1.0,
            )

        bi_ps = ps.tile([P, 2, P], F32, name="bi_ps")
        for c in range(2):
            nc.tensor.transpose(bi_ps[:, c, :], bi_col[:, c : c + 1].to_broadcast([P, P]), ident[:])

        def quantize(z):
            nc.vector.quantize_mx(
                out=wb_w[z][:].bitcast(E4M3), scales=wb_s[z][:], in_=wb_bf[z][:].rearrange("p n t -> p (n t)")
            )

        for z in range(PASSES):
            for a in range(2):
                nc.vector.tensor_copy(out=gs[a][z][:], in_=xs[:, z, :].indirect(lists[a][:]))
        for a in range(2):
            nc.vector.tensor_copy(out=gw[0][:, a, :], in_=xw[0][:].indirect(lists[a][:]))
        quantize(0)
        bi_row = sb.tile([P, P, 2], F32, name="bi_row", tag="wb_bf0", align_bytes=64)
        nc.scalar.activation(out=bi_row[:], in_=bi_ps[:].rearrange("p c q -> p q c"), func=ACT.Copy, scale=0.6)
        quantize(1)
        gw.append(sb.tile([P, 2, J], U32, name="gw1", tag="wb_raw1", align_bytes=64))
        for jt in range(JT):
            for a in (1, 0):
                nc.vector.tensor_copy(
                    out=gw[1][:, a, jt * P : (jt + 1) * P], in_=xw[1][:].indirect(lists[a][:, jt * 8 : (jt + 1) * 8])
                )

        acc = [ps.tile([P, N], F32, name=f"acc{jt}") for jt in range(JT)]

        def product(jt, a, z, start, stop):
            cols = slice(jt * P, (jt + 1) * P)
            if a == 0:
                rhs, rhs_scale = wa_w[z][:].bitcast(E5M2), wa_s[:, z, :]
            else:
                rhs, rhs_scale = wb_w[z][:].bitcast(E4M3), wb_s[z][:]
            nc.tensor.matmul_mx(
                out=acc[jt][:], lhsT=gw[z][:, a, cols].bitcast(E5M2), lhsT_scale=gs[a][z][:, cols],
                rhs=rhs, rhs_scale=rhs_scale, start=start, stop=stop,
            )

        for jt in range(JT):
            product(jt, 0, 0, True, False)
        for jt in range(JT):
            product(jt, 1, 0, False, False)
        for jt in range(JT):
            product(jt, 1, 1, False, False)
            product(jt, 0, 1, False, True)

        for jt in range(JT):
            neg = sb.tile([P, N], F32, name=f"neg{jt}")
            low = sb.tile([P, 1], F32, name=f"low{jt}")
            e = sb.tile([P, N], F32, name=f"e{jt}")
            total = sb.tile([P, 1], F32, name=f"total{jt}")
            inv = sb.tile([P, 1], F32, name=f"inv{jt}")
            y = sb.tile([P, N], F32, name=f"y{jt}")
            nc.vector.scalar_tensor_tensor(
                out=neg[:], in0=acc[jt][:], scalar=-0.6, in1=bi_row[:].rearrange("p q c -> p (q c)"),
                op0=ALU.mult, op1=ALU.add,
            )
            nc.vector.tensor_reduce(out=low[:], in_=neg[:], axis=mybir.AxisListType.X, op=ALU.min)
            nc.scalar.activation(out=e[:], in_=neg[:], func=ACT.Exp, bias=low[:], scale=-1.0, accum_out=total[:])
            nc.vector.reciprocal(out=inv[:], in_=total[:])
            nc.vector.tensor_scalar(out=y[:], in0=e[:], scalar1=inv[:], scalar2=256.0, op0=ALU.mult, op1=ALU.mult)
            queue = nc.sync if jt == 0 else nc.scalar
            queue.dma_start(out=out[jt * P : (jt + 1) * P, :], in_=y[:])
